import numpy as np
import ml_dtypes


def mxq(x, axis, fmt="e4m3"):
    dtype, down = {"e4m3": (ml_dtypes.float8_e4m3fn, 7), "e5m2": (ml_dtypes.float8_e5m2, 14)}[fmt]
    v = np.moveaxis(np.asarray(x, np.float32).astype(ml_dtypes.bfloat16).astype(np.float64), axis, -1)
    blocks = v.reshape(v.shape[:-1] + (-1, 32))
    amax = np.abs(blocks).max(-1, keepdims=True)
    byte = np.maximum(np.where(amax > 0, np.frexp(amax)[1] - 1 + 127, 0) - down, 1)
    scale = np.exp2(byte - 127.0)
    codes = (blocks / scale).astype(np.float32).astype(dtype).astype(np.float64)
    return np.moveaxis((codes * scale).reshape(v.shape), -1, axis)


WIDE = False


def mx_kscale(k):
    if not WIDE:
        return np.ones(k)
    levels = np.array([10, -10, 5, -5, 0])
    if k % 512:
        return np.exp2(np.random.permutation(np.resize(levels, k // 32))).repeat(32)
    a = np.empty((k // 512, 16))
    for p in range(k // 512):
        a[p, :8] = np.random.permutation(np.resize(levels, 8))
        for g in range(8):
            far = levels[np.abs(levels - a[p, g]) >= 10]
            a[p, g + 8] = far[np.random.randint(len(far))]
    return np.exp2(a.ravel()).repeat(32)


def f64(x):
    return np.asarray(x).astype(np.float64)


def striped(idx):
    return np.tile(idx.reshape(-1, 16).T, (8, 1)).astype(np.uint16)


def unstriped(offs):
    return offs[:16].T.reshape(-1).astype(np.int64)


E2M1 = np.array([0.0, 0.5, 1.0, 1.5, 2.0, 3.0, 4.0, 6.0, -0.0, -0.5, -1.0, -1.5, -2.0, -3.0, -4.0, -6.0])


def pack_weight(w, fmt):
    k, n = w.shape
    w = f64(np.asarray(w, np.float32).astype(ml_dtypes.bfloat16)).reshape(k // 32, 32, n)
    amax = np.abs(w).max(1)
    if fmt == "e4m3":
        byte = np.frexp(amax)[1] - 1 + 127 - 7
    else:
        mant, ex = np.frexp(amax / 6.0)
        byte = np.where(mant > 0.5, ex, ex - 1) + 127
    byte = np.clip(np.where(amax > 0, byte, 1), 1, 254)
    scaled = (w * np.exp2(127.0 - byte)[:, None, :]).reshape(k, n).astype(np.float32)
    by_word = np.ascontiguousarray(scaled.reshape(k // 512, 128, 4, n).transpose(0, 1, 3, 2))
    if fmt == "e4m3":
        words = by_word.astype(ml_dtypes.float8_e4m3fn).view(np.uint8)
    else:
        c = by_word.astype(ml_dtypes.float4_e2m1fn).view(np.uint8) & 0xF
        words = (c[..., 0::2] | (c[..., 1::2] << 4)).reshape(k // 512, 128, 2 * n)
    return np.ascontiguousarray(words), np.ascontiguousarray(byte.astype(np.uint8).reshape(k // 512, 16, n))


def unpack_weight(words, scales, fmt):
    g, _, n = scales.shape
    words = np.ascontiguousarray(words).reshape(g, 128, n, -1)
    if fmt == "e4m3":
        vals = words.view(ml_dtypes.float8_e4m3fn).astype(np.float64)
    else:
        nib = np.empty((g, 128, n, 4), np.uint8)
        nib[..., 0::2] = words & 0xF
        nib[..., 1::2] = words >> 4
        vals = E2M1[nib]
    vals = vals * np.repeat(np.exp2(scales.astype(np.float64) - 127.0), 8, axis=1)[..., None]
    return vals.transpose(0, 1, 3, 2).reshape(g * 512, n)


def gelu(v):
    return 0.5 * v * (1.0 + np.tanh(np.sqrt(2.0 / np.pi) * (v + 0.044715 * v**3)))


K, T, E, C, H, N = 512, 512, 4, 128, 512, 256


def by_expert(wq, xq):
    return np.concatenate([wq[e].T @ xq[:, e * C:(e + 1) * C] for e in range(E)], axis=1)


def setup_inputs():
    n = np.random.standard_normal
    s = mx_kscale(K)[:, None]
    u = mx_kscale(H)
    w1 = [pack_weight(m, "e2m1") for m in n((E + 1, K, H)) / np.sqrt(K) / s[None]]
    w3 = [pack_weight(m, "e2m1") for m in n((E + 1, K, H)) / np.sqrt(K) / s[None] * u[None, None, :]]
    w2 = [pack_weight(m, "e2m1") for m in n((E + 1, H, N)) / np.sqrt(H) / u[None, :, None]]
    return {
        "xT": (n((K, T)) * s).astype(np.float32),
        "w1_words": np.stack([m[0] for m in w1]),
        "w1_scales": np.stack([m[1] for m in w1]),
        "w3_words": np.stack([m[0] for m in w3]),
        "w3_scales": np.stack([m[1] for m in w3]),
        "w2_words": np.stack([m[0] for m in w2]),
        "w2_scales": np.stack([m[1] for m in w2]),
        "gate": np.tile(np.random.uniform(0.2, 1.0, E * C), (N, 1)).astype(np.float32),
        "offs": striped(np.random.permutation(T)[:E * C]),
    }


def reference(xT, w1_words, w1_scales, w3_words, w3_scales, w2_words, w2_scales, gate, offs):
    idx = unstriped(offs)
    w1 = np.stack([unpack_weight(w1_words[e], w1_scales[e], "e2m1") for e in range(E + 1)])
    w3 = np.stack([unpack_weight(w3_words[e], w3_scales[e], "e2m1") for e in range(E + 1)])
    w2 = np.stack([unpack_weight(w2_words[e], w2_scales[e], "e2m1") for e in range(E + 1)])
    w1q, w3q, w2q = w1, w3, w2
    xs = mxq(f64(xT), 0, "e4m3")
    hs = gelu(w1q[E].T @ xs) * (w3q[E].T @ xs)
    ys = w2q[E].T @ mxq(hs, 0, "e4m3")
    xq = mxq(f64(xT)[:, idx], 0, "e4m3")
    h = gelu(by_expert(w1q, xq))
    h = h * by_expert(w3q, xq)
    y = by_expert(w2q, mxq(h, 0, "e4m3"))
    out = ys
    out[:, idx] += f64(gate) * y
    return out

@@ -1,0 +1,223 @@
+from contextlib import ExitStack
+
+import concourse.mybir as mybir
+from concourse.masks import make_identity
+
+K, T, E, C, H, N = 512, 512, 4, 128, 512, 256
+FLOPS = 2 * 2 * T * (2 * K * H + H * N)
+
+F32 = mybir.dt.float32
+BF16 = mybir.dt.bfloat16
+I32 = mybir.dt.int32
+U32 = mybir.dt.uint32
+U16 = mybir.dt.uint16
+U8 = mybir.dt.uint8
+FP8X4 = mybir.dt.float8_e4m3fn_x4
+FP4X4 = mybir.dt.float4_e2m1fn_x4
+GELU = mybir.ActivationFunctionType.Gelu_apprx_tanh
+MULT = mybir.AluOpType.mult
+ADD = mybir.AluOpType.add
+P = 128
+V_TOK = 336
+
+
+def tile_moe_shr_glu_gelu_kernel(
+    tc, xT, w1_words, w1_scales, w3_words, w3_scales, w2_words, w2_scales, gate, offs, out
+):
+    nc = tc.nc
+    with ExitStack() as ctx:
+        keep = ctx.enter_context(tc.tile_pool(name="keep", bufs=1))
+        work = ctx.enter_context(tc.tile_pool(name="work", bufs=2))
+        psum = ctx.enter_context(tc.psum_pool(name="psum", bufs=2))
+
+        offsets = keep.tile([P, T // 16], U16, name="offsets")
+        nc.sync.dma_start(offsets[:], offs)
+
+        x_rows = xT.rearrange("(p j) t -> p j t", j=4)
+        x_raw = [keep.tile([P, 2, T], F32, name="x_raw%d" % u) for u in range(2)]
+        for u in range(2):
+            nc.sync.dma_start(x_raw[u][:], x_rows[:, 2 * u : 2 * u + 2, :])
+
+        warm = keep.tile([P, 1], F32, name="warm")
+        nc.vector.memset(warm[:], 0.0)
+        warm_out = keep.tile([P, 1], F32, name="warm_out")
+
+        w1s = keep.tile([P, 5 * H], U8, name="w1s", align_bytes=64)
+        w3s = keep.tile([P, 5 * H], U8, name="w3s", align_bytes=64)
+        w2s = keep.tile([P, 5 * N], U8, name="w2s", align_bytes=64)
+        nc.vector.memset(w1s[:].bitcast(I32), 0)
+        nc.vector.memset(w3s[:].bitcast(I32), 0)
+        nc.gpsimd.memset(w2s[:].bitcast(I32), 0)
+
+        def load_scales(queue, plane, scales):
+            src = scales[:, 0].rearrange("e (q r) i -> r q e i", r=4)
+            dst = plane[:].bitcast(I32)
+            for r in range(4):
+                queue.dma_start(
+                    dst[r:P:32, :].rearrange("q (e i) -> q e i", e=5), src[r].bitcast(I32)
+                )
+
+        load_scales(nc.scalar, w1s, w1_scales)
+        load_scales(nc.scalar, w3s, w3_scales)
+        nc.scalar.activation(warm_out[:], warm[:], GELU)
+        load_scales(nc.gpsimd, w2s, w2_scales)
+
+        ident = keep.tile([P, P], F32, name="ident")
+        make_identity(nc, ident[:])
+
+        w1w = keep.tile([P, 5, 2 * H], U8, name="w1w", align_bytes=64)
+        w3w = keep.tile([P, 5, 2 * H], U8, name="w3w", align_bytes=64)
+        w2w = keep.tile([P, 5, 2 * N], U8, name="w2w", align_bytes=64)
+
+        def load_words(tile, words, lo, hi):
+            nc.sync.dma_start(
+                tile[:, lo:hi, :].bitcast(I32), words[lo:hi, 0].rearrange("e p b -> p e b").bitcast(I32)
+            )
+
+        load_words(w1w, w1_words, 0, 1)
+        load_words(w3w, w3_words, 0, 1)
+        load_words(w1w, w1_words, 4, 5)
+        load_words(w3w, w3_words, 4, 5)
+        load_words(w2w, w2_words, 0, 5)
+        gates = keep.tile([P, T], F32, name="gates")
+        load_words(w1w, w1_words, 1, 2)
+        load_words(w3w, w3_words, 1, 2)
+        nc.sync.dma_start(gates[:], gate[0:P, :])
+        load_words(w1w, w1_words, 2, 4)
+        load_words(w3w, w3_words, 2, 4)
+
+        x_pair = [keep.tile([P, T, 2], BF16, name="x_pair%d" % u) for u in range(2)]
+        for u in range(2):
+            for eng, lo, hi in ((nc.vector.tensor_copy, 0, V_TOK), (nc.scalar.copy, V_TOK, T)):
+                eng(x_pair[u][:, lo:hi, :], x_raw[u][:, :, lo:hi].rearrange("p e t -> p t e"))
+
+        x_slot = [keep.tile([P, C, 4], BF16, name="x_slot%d" % c, align_bytes=64) for c in range(E)]
+        x_codes = [keep.tile([P, C], U32, name="x_codes%d" % c, align_bytes=64) for c in range(E)]
+        x_scales = [keep.tile([P, C], U8, name="x_scales%d" % c, align_bytes=64) for c in range(E)]
+        window = [keep.tile([P, T], F32, name="window%d" % u) for u in range(2)]
+
+        def gather(c, u):
+            words = x_slot[c][:].rearrange("p s d -> p (s d)").bitcast(U32)
+            nc.vector.tensor_copy(
+                words.rearrange("p (s u) -> p u s", u=2)[:, u, :],
+                x_pair[u][:].rearrange("p t e -> p (t e)").bitcast(U32).indirect(offsets[:, 8 * c : 8 * c + 8]),
+            )
+
+        def quant_x(c):
+            nc.vector.quantize_mx(
+                out=x_codes[c][:].bitcast(FP8X4), scales=x_scales[c][:], in_=x_slot[c][:].rearrange("p s d -> p (s d)")
+            )
+
+        hidden, h_codes, h_scales, banks, results = {}, {}, {}, {}, {}
+
+        def project(c, sub):
+            e = (c, E)[sub]
+            a = psum.tile([P, H], F32, name="a")
+            b = psum.tile([P, H], F32, name="b")
+            for bank, words, scales in ((a, w1w, w1s), (b, w3w, w3s)):
+                nc.tensor.matmul_mx(
+                    out=bank[:],
+                    lhsT=x_codes[c][:].bitcast(FP8X4),
+                    lhsT_scale=x_scales[c][:],
+                    rhs=words[:, e, :].bitcast(FP4X4),
+                    rhs_scale=scales[:, e * H : (e + 1) * H],
+                    start=True,
+                    stop=True,
+                )
+            banks[c, sub] = (a, b)
+
+        def glu(c, sub):
+            a, b = banks[c, sub]
+            if sub == 0:
+                hidden[c] = work.tile([P, 2, 2, P, 2], BF16, name="hidden", align_bytes=64)
+            g = work.tile([P, 2, P, 2], F32, name="g")
+            nc.scalar.activation(g[:], a[:].rearrange("s (q u e) -> s u q e", u=2, e=2), GELU)
+            nc.vector.tensor_tensor(hidden[c][:, sub], g[:], b[:].rearrange("s (q u e) -> s u q e", u=2, e=2), MULT)
+
+        def turn(c):
+            t = psum.tile([P, 2, 2, C], F32, name="t")
+            words = hidden[c][:].rearrange("s b u q e -> s (b u q e)").bitcast(F32)
+            for sub in range(2):
+                for u in range(2):
+                    k = (2 * sub + u) * P
+                    nc.tensor.transpose(t[:, sub, u, :], words[:, k : k + P], ident[:])
+            grouped = work.tile([P, 2, C, 4], BF16, name="grouped", align_bytes=64)
+            nc.scalar.copy(
+                grouped[:].rearrange("p b s d -> p (b s d)").bitcast(F32).rearrange("p (b s u) -> p b s u", b=2, u=2),
+                t[:].rearrange("p b u s -> p b s u"),
+            )
+            h_codes[c] = (grouped,)
+
+        def quant_h(c):
+            (grouped,) = h_codes[c]
+            codes = work.tile([P, 2 * C], U32, name="h_code", align_bytes=64)
+            scales = work.tile([P, 2 * C], U8, name="h_scale", align_bytes=64)
+            nc.vector.quantize_mx(
+                out=codes[:].bitcast(FP8X4), scales=scales[:], in_=grouped[:].rearrange("p b s d -> p (b s d)")
+            )
+            h_codes[c] = (codes, scales)
+
+        def last_layer(c):
+            codes, scales = h_codes[c]
+            y = psum.tile([P, 2, 2, C], F32, name="y")
+            for sub in range(2):
+                e = (c, E)[sub]
+                for u in range(2):
+                    nc.tensor.matmul_mx(
+                        out=y[:, sub, u, :],
+                        lhsT=w2w[:, e, 2 * u * P : 2 * (u + 1) * P].bitcast(FP4X4),
+                        lhsT_scale=w2s[:, e * N + u * P : e * N + (u + 1) * P],
+                        rhs=codes[:, sub * C : (sub + 1) * C].bitcast(FP8X4),
+                        rhs_scale=scales[:, sub * C : (sub + 1) * C],
+                        start=True,
+                        stop=True,
+                    )
+            results[c] = y
+
+        def combine(c):
+            y = results[c]
+            gated = work.tile([P, 2, C], F32, name="gated")
+            gcol = gates[:, c * C : (c + 1) * C].unsqueeze(1).to_broadcast([P, 2, C])
+            nc.vector.tensor_tensor(gated[:], y[:, 0], gcol, MULT)
+            total = work.tile([P, 2, C], F32, name="total")
+            nc.vector.tensor_tensor(total[:], gated[:], y[:, 1], ADD)
+            results[c] = total
+
+        def scatter(c):
+            for u in range(2):
+                nc.vector.tensor_copy(window[u][:].indirect(offsets[:, 8 * c : 8 * c + 8]), results[c][:, u, :])
+
+        for c in range(3):
+            gather(c, 0)
+        gather(0, 1)
+        gather(1, 1)
+        quant_x(0)
+        project(0, 0)
+        gather(2, 1)
+        quant_x(1)
+        project(0, 1)
+        gather(3, 0)
+        gather(3, 1)
+        quant_x(2)
+        glu(0, 0)
+        project(1, 0)
+        glu(0, 1)
+        quant_x(3)
+        for c in range(E):
+            turn(c)
+            if c + 1 < E:
+                project(c + 1, 1)
+                glu(c + 1, 0)
+                quant_h(c)
+                if c + 2 < E:
+                    project(c + 2, 0)
+                glu(c + 1, 1)
+            else:
+                quant_h(c)
+            last_layer(c)
+            if c > 0:
+                scatter(c - 1)
+            combine(c)
+        scatter(E - 1)
+        for u in range(2):
+            nc.sync.dma_start(out[u * P : (u + 1) * P, :], window[u][:])

@@ -18,7 +18,8 @@ GELU = mybir.ActivationFunctionType.Gelu_apprx_tanh
 MULT = mybir.AluOpType.mult
 ADD = mybir.AluOpType.add
 P = 128
-V_TOK = 336
+GP = ()
+V_TOK = (336, 336)
 
 
 def tile_moe_shr_glu_gelu_kernel(
@@ -35,9 +36,11 @@ def tile_moe_shr_glu_gelu_kernel(
 
         x_rows = xT.rearrange("(p j) t -> p j t", j=4)
         x_raw = [keep.tile([P, 2, T], F32, name="x_raw%d" % u) for u in range(2)]
-        for u in range(2):
+
+        def load_x(u):
             nc.sync.dma_start(x_raw[u][:], x_rows[:, 2 * u : 2 * u + 2, :])
 
+        load_x(0)
         warm = keep.tile([P, 1], F32, name="warm")
         nc.vector.memset(warm[:], 0.0)
         warm_out = keep.tile([P, 1], F32, name="warm_out")
@@ -45,58 +48,59 @@ def tile_moe_shr_glu_gelu_kernel(
         w1s = keep.tile([P, 5 * H], U8, name="w1s", align_bytes=64)
         w3s = keep.tile([P, 5 * H], U8, name="w3s", align_bytes=64)
         w2s = keep.tile([P, 5 * N], U8, name="w2s", align_bytes=64)
-        nc.vector.memset(w1s[:].bitcast(I32), 0)
+        nc.gpsimd.memset(w1s[:].bitcast(I32), 0)
         nc.vector.memset(w3s[:].bitcast(I32), 0)
-        nc.gpsimd.memset(w2s[:].bitcast(I32), 0)
+        nc.vector.memset(w2s[:].bitcast(I32), 0)
+        ident = keep.tile([P, P], F32, name="ident")
+        make_identity(nc, ident[:])
+        nc.scalar.activation(warm_out[:], warm[:], GELU)
 
-        def load_scales(queue, plane, scales):
+        def load_scales(queue, plane, scales, rows):
             src = scales[:, 0].rearrange("e (q r) i -> r q e i", r=4)
             dst = plane[:].bitcast(I32)
-            for r in range(4):
+            for r in rows:
                 queue.dma_start(
                     dst[r:P:32, :].rearrange("q (e i) -> q e i", e=5), src[r].bitcast(I32)
                 )
-
-        load_scales(nc.scalar, w1s, w1_scales)
-        load_scales(nc.scalar, w3s, w3_scales)
-        nc.scalar.activation(warm_out[:], warm[:], GELU)
-        load_scales(nc.gpsimd, w2s, w2_scales)
-
-        ident = keep.tile([P, P], F32, name="ident")
-        make_identity(nc, ident[:])
 
         w1w = keep.tile([P, 5, 2 * H], U8, name="w1w", align_bytes=64)
         w3w = keep.tile([P, 5, 2 * H], U8, name="w3w", align_bytes=64)
         w2w = keep.tile([P, 5, 2 * N], U8, name="w2w", align_bytes=64)
 
-        def load_words(tile, words, lo, hi):
-            nc.sync.dma_start(
+        def load_words(tile, words, lo, hi, queue=nc.sync):
+            queue.dma_start(
                 tile[:, lo:hi, :].bitcast(I32), words[lo:hi, 0].rearrange("e p b -> p e b").bitcast(I32)
             )
 
-        load_words(w1w, w1_words, 0, 1)
-        load_words(w3w, w3_words, 0, 1)
-        load_words(w1w, w1_words, 4, 5)
-        load_words(w3w, w3_words, 4, 5)
-        load_words(w2w, w2_words, 0, 5)
-        gates = keep.tile([P, T], F32, name="gates")
+        load_x(1)
+        load_words(w1w, w1_words, 0, 1, nc.gpsimd)
+        load_words(w3w, w3_words, 0, 1, nc.gpsimd)
+        load_words(w1w, w1_words, 4, 5, nc.gpsimd)
+        load_words(w3w, w3_words, 4, 5, nc.gpsimd)
+        load_scales(nc.sync, w1s, w1_scales, (0, 1, 2, 3))
+        load_scales(nc.sync, w3s, w3_scales, (0, 1, 2, 3))
         load_words(w1w, w1_words, 1, 2)
         load_words(w3w, w3_words, 1, 2)
+        load_words(w2w, w2_words, 0, 5)
+        load_scales(nc.sync, w2s, w2_scales, (0, 1, 2, 3))
+        gates = keep.tile([P, T], F32, name="gates")
         nc.sync.dma_start(gates[:], gate[0:P, :])
         load_words(w1w, w1_words, 2, 4)
         load_words(w3w, w3_words, 2, 4)
 
         x_pair = [keep.tile([P, T, 2], BF16, name="x_pair%d" % u) for u in range(2)]
         for u in range(2):
-            for eng, lo, hi in ((nc.vector.tensor_copy, 0, V_TOK), (nc.scalar.copy, V_TOK, T)):
+            for eng, lo, hi in ((nc.vector.tensor_copy, 0, V_TOK[u]), (nc.scalar.copy, V_TOK[u], T)):
                 eng(x_pair[u][:, lo:hi, :], x_raw[u][:, :, lo:hi].rearrange("p e t -> p t e"))
 
-        x_slot = [keep.tile([P, C, 4], BF16, name="x_slot%d" % c, align_bytes=64) for c in range(E)]
-        x_codes = [keep.tile([P, C], U32, name="x_codes%d" % c, align_bytes=64) for c in range(E)]
-        x_scales = [keep.tile([P, C], U8, name="x_scales%d" % c, align_bytes=64) for c in range(E)]
+        x_slot = {}
+        x_codes = keep.tile([P, T], U32, name="x_codes", align_bytes=64)
+        x_scales = keep.tile([P, T], U8, name="x_scales", align_bytes=64)
         window = [keep.tile([P, T], F32, name="window%d" % u) for u in range(2)]
 
         def gather(c, u):
+            if u == 0:
+                x_slot[c] = work.tile([P, C, 4], BF16, name="x_slot", align_bytes=64)
             words = x_slot[c][:].rearrange("p s d -> p (s d)").bitcast(U32)
             nc.vector.tensor_copy(
                 words.rearrange("p (s u) -> p u s", u=2)[:, u, :],
@@ -105,7 +109,9 @@ def tile_moe_shr_glu_gelu_kernel(
 
         def quant_x(c):
             nc.vector.quantize_mx(
-                out=x_codes[c][:].bitcast(FP8X4), scales=x_scales[c][:], in_=x_slot[c][:].rearrange("p s d -> p (s d)")
+                out=x_codes[:, c * C : (c + 1) * C].bitcast(FP8X4),
+                scales=x_scales[:, c * C : (c + 1) * C],
+                in_=x_slot[c][:].rearrange("p s d -> p (s d)"),
             )
 
         hidden, h_codes, h_scales, banks, results = {}, {}, {}, {}, {}
@@ -117,8 +123,8 @@ def tile_moe_shr_glu_gelu_kernel(
             for bank, words, scales in ((a, w1w, w1s), (b, w3w, w3s)):
                 nc.tensor.matmul_mx(
                     out=bank[:],
-                    lhsT=x_codes[c][:].bitcast(FP8X4),
-                    lhsT_scale=x_scales[c][:],
+                    lhsT=x_codes[:, c * C : (c + 1) * C].bitcast(FP8X4),
+                    lhsT_scale=x_scales[:, c * C : (c + 1) * C],
                     rhs=words[:, e, :].bitcast(FP4X4),
                     rhs_scale=scales[:, e * H : (e + 1) * H],
                     start=True,
@@ -134,87 +140,103 @@ def tile_moe_shr_glu_gelu_kernel(
             nc.scalar.activation(g[:], a[:].rearrange("s (q u e) -> s u q e", u=2, e=2), GELU)
             nc.vector.tensor_tensor(hidden[c][:, sub], g[:], b[:].rearrange("s (q u e) -> s u q e", u=2, e=2), MULT)
 
-        def turn(c):
-            t = psum.tile([P, 2, 2, C], F32, name="t")
+        def turn(c, lo, hi):
+            m = hi - lo
+            t = psum.tile([P, m, 2, C], F32, name="t")
             words = hidden[c][:].rearrange("s b u q e -> s (b u q e)").bitcast(F32)
-            for sub in range(2):
+            for sub in range(lo, hi):
                 for u in range(2):
                     k = (2 * sub + u) * P
-                    nc.tensor.transpose(t[:, sub, u, :], words[:, k : k + P], ident[:])
-            grouped = work.tile([P, 2, C, 4], BF16, name="grouped", align_bytes=64)
+                    nc.tensor.transpose(t[:, sub - lo, u, :], words[:, k : k + P], ident[:])
+            grouped = work.tile([P, m, C, 4], BF16, name="grouped%d" % m, align_bytes=64)
             nc.scalar.copy(
-                grouped[:].rearrange("p b s d -> p (b s d)").bitcast(F32).rearrange("p (b s u) -> p b s u", b=2, u=2),
+                grouped[:].rearrange("p b s d -> p (b s d)").bitcast(F32).rearrange("p (b s u) -> p b s u", b=m, u=2),
                 t[:].rearrange("p b u s -> p b s u"),
             )
-            h_codes[c] = (grouped,)
+            h_codes[c, lo] = grouped
 
-        def quant_h(c):
-            (grouped,) = h_codes[c]
-            codes = work.tile([P, 2 * C], U32, name="h_code", align_bytes=64)
-            scales = work.tile([P, 2 * C], U8, name="h_scale", align_bytes=64)
+        def quant_h(c, lo, hi):
+            m = hi - lo
+            codes = work.tile([P, m * C], U32, name="h_code%d" % m, align_bytes=64)
+            scales = work.tile([P, m * C], U8, name="h_scale%d" % m, align_bytes=64)
             nc.vector.quantize_mx(
-                out=codes[:].bitcast(FP8X4), scales=scales[:], in_=grouped[:].rearrange("p b s d -> p (b s d)")
+                out=codes[:].bitcast(FP8X4),
+                scales=scales[:],
+                in_=h_codes[c, lo][:].rearrange("p b s d -> p (b s d)"),
             )
-            h_codes[c] = (codes, scales)
+            for sub in range(lo, hi):
+                k = (sub - lo) * C
+                h_codes[c, sub] = (codes[:, k : k + C], scales[:, k : k + C])
 
-        def last_layer(c):
-            codes, scales = h_codes[c]
-            y = psum.tile([P, 2, 2, C], F32, name="y")
-            for sub in range(2):
+        def last_layer(c, lo, hi):
+            if lo == 0:
+                results[c] = psum.tile([P, 2, 2, C], F32, name="y")
+            y = results[c]
+            for sub in range(lo, hi):
                 e = (c, E)[sub]
+                codes, scales = h_codes[c, sub]
                 for u in range(2):
                     nc.tensor.matmul_mx(
                         out=y[:, sub, u, :],
                         lhsT=w2w[:, e, 2 * u * P : 2 * (u + 1) * P].bitcast(FP4X4),
                         lhsT_scale=w2s[:, e * N + u * P : e * N + (u + 1) * P],
-                        rhs=codes[:, sub * C : (sub + 1) * C].bitcast(FP8X4),
-                        rhs_scale=scales[:, sub * C : (sub + 1) * C],
+                        rhs=codes.bitcast(FP8X4),
+                        rhs_scale=scales,
                         start=True,
                         stop=True,
                     )
-            results[c] = y
 
         def combine(c):
             y = results[c]
-            gated = work.tile([P, 2, C], F32, name="gated")
             gcol = gates[:, c * C : (c + 1) * C].unsqueeze(1).to_broadcast([P, 2, C])
-            nc.vector.tensor_tensor(gated[:], y[:, 0], gcol, MULT)
-            total = work.tile([P, 2, C], F32, name="total")
-            nc.vector.tensor_tensor(total[:], gated[:], y[:, 1], ADD)
+            gated = work.tile([P, 2, C], F32, name="gated")
+            total = keep.tile([P, 2, C], F32, name="total%d" % c)
+            if c in GP:
+                y_sb = work.tile([P, 2, 2, C], F32, name="y_sb")
+                nc.scalar.copy(y_sb[:], y[:])
+                nc.gpsimd.tensor_tensor(gated[:], y_sb[:, 0], gcol, MULT)
+                nc.gpsimd.tensor_tensor(total[:], gated[:], y_sb[:, 1], ADD)
+            else:
+                nc.vector.tensor_tensor(gated[:], y[:, 0], gcol, MULT)
+                nc.vector.tensor_tensor(total[:], gated[:], y[:, 1], ADD)
             results[c] = total
 
         def scatter(c):
             for u in range(2):
                 nc.vector.tensor_copy(window[u][:].indirect(offsets[:, 8 * c : 8 * c + 8]), results[c][:, u, :])
 
-        for c in range(3):
-            gather(c, 0)
+        gather(0, 0)
+        gather(1, 0)
         gather(0, 1)
         gather(1, 1)
         quant_x(0)
-        project(0, 0)
-        gather(2, 1)
         quant_x(1)
-        project(0, 1)
+        gather(2, 0)
+        gather(2, 1)
+        quant_x(2)
         gather(3, 0)
         gather(3, 1)
-        quant_x(2)
+        quant_x(3)
+        project(0, 0)
+        project(0, 1)
         glu(0, 0)
         project(1, 0)
         glu(0, 1)
-        quant_x(3)
         for c in range(E):
-            turn(c)
+            pieces = ((0, 2),) if c < E - 1 else ((0, 1), (1, 2))
+            for lo, hi in pieces:
+                turn(c, lo, hi)
             if c + 1 < E:
                 project(c + 1, 1)
                 glu(c + 1, 0)
-                quant_h(c)
-                if c + 2 < E:
-                    project(c + 2, 0)
+            for lo, hi in pieces:
+                quant_h(c, lo, hi)
+            if c + 2 < E:
+                project(c + 2, 0)
+            if c + 1 < E:
                 glu(c + 1, 1)
-            else:
-                quant_h(c)
-            last_layer(c)
+            for lo, hi in pieces:
+                last_layer(c, lo, hi)
             if c > 0:
                 scatter(c - 1)
             combine(c)

@@ -19,7 +19,7 @@ MULT = mybir.AluOpType.mult
 ADD = mybir.AluOpType.add
 P = 128
 GP = ()
-V_TOK = (336, 336)
+V_TOK = (0, 128)
 
 
 def tile_moe_shr_glu_gelu_kernel(
@@ -52,7 +52,6 @@ def tile_moe_shr_glu_gelu_kernel(
         nc.vector.memset(w3s[:].bitcast(I32), 0)
         nc.vector.memset(w2s[:].bitcast(I32), 0)
         ident = keep.tile([P, P], F32, name="ident")
-        make_identity(nc, ident[:])
         nc.scalar.activation(warm_out[:], warm[:], GELU)
 
         def load_scales(queue, plane, scales, rows):
@@ -67,31 +66,33 @@ def tile_moe_shr_glu_gelu_kernel(
         w3w = keep.tile([P, 5, 2 * H], U8, name="w3w", align_bytes=64)
         w2w = keep.tile([P, 5, 2 * N], U8, name="w2w", align_bytes=64)
 
-        def load_words(tile, words, lo, hi, queue=nc.sync):
+        def load_words(queue, tile, words, experts):
             queue.dma_start(
-                tile[:, lo:hi, :].bitcast(I32), words[lo:hi, 0].rearrange("e p b -> p e b").bitcast(I32)
+                tile[:, experts, :].bitcast(I32), words[experts, 0].rearrange("e p b -> p e b").bitcast(I32)
             )
 
+        gates = keep.tile([P, T], F32, name="gates")
+        for tile in (w1w[:, 1, 0:4], w3w[:, 1, 0:4], w2w[:, 0, 0:4]):
+            nc.vector.memset(tile.bitcast(I32), 0)
+        nc.vector.memset(gates[:, 0:1], 0.0)
+        load_words(nc.gpsimd, w1w, w1_words, slice(0, 5, 4))
+        load_words(nc.gpsimd, w3w, w3_words, slice(0, 5, 4))
+        make_identity(nc, ident[:])
         load_x(1)
-        load_words(w1w, w1_words, 0, 1, nc.gpsimd)
-        load_words(w3w, w3_words, 0, 1, nc.gpsimd)
-        load_words(w1w, w1_words, 4, 5, nc.gpsimd)
-        load_words(w3w, w3_words, 4, 5, nc.gpsimd)
         load_scales(nc.sync, w1s, w1_scales, (0, 1, 2, 3))
         load_scales(nc.sync, w3s, w3_scales, (0, 1, 2, 3))
-        load_words(w1w, w1_words, 1, 2)
-        load_words(w3w, w3_words, 1, 2)
-        load_words(w2w, w2_words, 0, 5)
+        load_words(nc.sync, w1w, w1_words, slice(1, 4))
+        load_words(nc.sync, w3w, w3_words, slice(1, 4))
+        load_words(nc.sync, w2w, w2_words, slice(0, 5))
         load_scales(nc.sync, w2s, w2_scales, (0, 1, 2, 3))
-        gates = keep.tile([P, T], F32, name="gates")
         nc.sync.dma_start(gates[:], gate[0:P, :])
-        load_words(w1w, w1_words, 2, 4)
-        load_words(w3w, w3_words, 2, 4)
 
         x_pair = [keep.tile([P, T, 2], BF16, name="x_pair%d" % u) for u in range(2)]
-        for u in range(2):
+
+        def cast(u):
             for eng, lo, hi in ((nc.vector.tensor_copy, 0, V_TOK[u]), (nc.scalar.copy, V_TOK[u], T)):
-                eng(x_pair[u][:, lo:hi, :], x_raw[u][:, :, lo:hi].rearrange("p e t -> p t e"))
+                if hi > lo:
+                    eng(x_pair[u][:, lo:hi, :], x_raw[u][:, :, lo:hi].rearrange("p e t -> p t e"))
 
         x_slot = {}
         x_codes = keep.tile([P, T], U32, name="x_codes", align_bytes=64)
@@ -101,6 +102,10 @@ def tile_moe_shr_glu_gelu_kernel(
         def gather(c, u):
             if u == 0:
                 x_slot[c] = work.tile([P, C, 4], BF16, name="x_slot", align_bytes=64)
+            if c == 0:
+                for e in range(2):
+                    nc.vector.tensor_copy(x_slot[c][:, :, 2 * u + e], x_raw[u][:, e, :].indirect(offsets[:, 0:8]))
+                return
             words = x_slot[c][:].rearrange("p s d -> p (s d)").bitcast(U32)
             nc.vector.tensor_copy(
                 words.rearrange("p (s u) -> p u s", u=2)[:, u, :],
@@ -206,10 +211,12 @@ def tile_moe_shr_glu_gelu_kernel(
                 nc.vector.tensor_copy(window[u][:].indirect(offsets[:, 8 * c : 8 * c + 8]), results[c][:, u, :])
 
         gather(0, 0)
-        gather(1, 0)
+        cast(0)
         gather(0, 1)
-        gather(1, 1)
+        cast(1)
         quant_x(0)
+        gather(1, 0)
+        gather(1, 1)
         quant_x(1)
         gather(2, 0)
         gather(2, 1)

from contextlib import ExitStack

import concourse.mybir as mybir
from concourse.masks import make_identity

K, T, E, C, H, N = 512, 512, 4, 128, 512, 256
FLOPS = 2 * 2 * T * (2 * K * H + H * N)

F32 = mybir.dt.float32
BF16 = mybir.dt.bfloat16
I32 = mybir.dt.int32
U32 = mybir.dt.uint32
U16 = mybir.dt.uint16
U8 = mybir.dt.uint8
FP8X4 = mybir.dt.float8_e4m3fn_x4
FP4X4 = mybir.dt.float4_e2m1fn_x4
GELU = mybir.ActivationFunctionType.Gelu_apprx_tanh
MULT = mybir.AluOpType.mult
ADD = mybir.AluOpType.add
P = 128
GP = ()
V_TOK = (0, 128)


def tile_moe_shr_glu_gelu_kernel(
    tc, xT, w1_words, w1_scales, w3_words, w3_scales, w2_words, w2_scales, gate, offs, out
):
    nc = tc.nc
    with ExitStack() as ctx:
        keep = ctx.enter_context(tc.tile_pool(name="keep", bufs=1))
        work = ctx.enter_context(tc.tile_pool(name="work", bufs=2))
        psum = ctx.enter_context(tc.psum_pool(name="psum", bufs=2))

        offsets = keep.tile([P, T // 16], U16, name="offsets")
        nc.sync.dma_start(offsets[:], offs)

        x_rows = xT.rearrange("(p j) t -> p j t", j=4)
        x_raw = [keep.tile([P, 2, T], F32, name="x_raw%d" % u) for u in range(2)]

        def load_x(u):
            nc.sync.dma_start(x_raw[u][:], x_rows[:, 2 * u : 2 * u + 2, :])

        load_x(0)
        warm = keep.tile([P, 1], F32, name="warm")
        nc.vector.memset(warm[:], 0.0)
        warm_out = keep.tile([P, 1], F32, name="warm_out")

        w1s = keep.tile([P, 5 * H], U8, name="w1s", align_bytes=64)
        w3s = keep.tile([P, 5 * H], U8, name="w3s", align_bytes=64)
        w2s = keep.tile([P, 5 * N], U8, name="w2s", align_bytes=64)
        nc.gpsimd.memset(w1s[:].bitcast(I32), 0)
        nc.vector.memset(w3s[:].bitcast(I32), 0)
        nc.vector.memset(w2s[:].bitcast(I32), 0)
        ident = keep.tile([P, P], F32, name="ident")
        nc.scalar.activation(warm_out[:], warm[:], GELU)

        def load_scales(queue, plane, scales, rows):
            src = scales[:, 0].rearrange("e (q r) i -> r q e i", r=4)
            dst = plane[:].bitcast(I32)
            for r in rows:
                queue.dma_start(
                    dst[r:P:32, :].rearrange("q (e i) -> q e i", e=5), src[r].bitcast(I32)
                )

        w1w = keep.tile([P, 5, 2 * H], U8, name="w1w", align_bytes=64)
        w3w = keep.tile([P, 5, 2 * H], U8, name="w3w", align_bytes=64)
        w2w = keep.tile([P, 5, 2 * N], U8, name="w2w", align_bytes=64)

        def load_words(queue, tile, words, experts):
            queue.dma_start(
                tile[:, experts, :].bitcast(I32), words[experts, 0].rearrange("e p b -> p e b").bitcast(I32)
            )

        gates = keep.tile([P, T], F32, name="gates")
        for tile in (w1w[:, 1, 0:4], w3w[:, 1, 0:4], w2w[:, 0, 0:4]):
            nc.vector.memset(tile.bitcast(I32), 0)
        nc.vector.memset(gates[:, 0:1], 0.0)
        load_words(nc.gpsimd, w1w, w1_words, slice(0, 5, 4))
        load_words(nc.gpsimd, w3w, w3_words, slice(0, 5, 4))
        make_identity(nc, ident[:])
        load_x(1)
        load_scales(nc.sync, w1s, w1_scales, (0, 1, 2, 3))
        load_scales(nc.sync, w3s, w3_scales, (0, 1, 2, 3))
        load_words(nc.sync, w1w, w1_words, slice(1, 4))
        load_words(nc.sync, w3w, w3_words, slice(1, 4))
        load_words(nc.sync, w2w, w2_words, slice(0, 5))
        load_scales(nc.sync, w2s, w2_scales, (0, 1, 2, 3))
        nc.sync.dma_start(gates[:], gate[0:P, :])

        x_pair = [keep.tile([P, T, 2], BF16, name="x_pair%d" % u) for u in range(2)]

        def cast(u):
            for eng, lo, hi in ((nc.vector.tensor_copy, 0, V_TOK[u]), (nc.scalar.copy, V_TOK[u], T)):
                if hi > lo:
                    eng(x_pair[u][:, lo:hi, :], x_raw[u][:, :, lo:hi].rearrange("p e t -> p t e"))

        x_slot = {}
        x_codes = keep.tile([P, T], U32, name="x_codes", align_bytes=64)
        x_scales = keep.tile([P, T], U8, name="x_scales", align_bytes=64)
        window = [keep.tile([P, T], F32, name="window%d" % u) for u in range(2)]

        def gather(c, u):
            if u == 0:
                x_slot[c] = work.tile([P, C, 4], BF16, name="x_slot", align_bytes=64)
            if c == 0:
                for e in range(2):
                    nc.vector.tensor_copy(x_slot[c][:, :, 2 * u + e], x_raw[u][:, e, :].indirect(offsets[:, 0:8]))
                return
            words = x_slot[c][:].rearrange("p s d -> p (s d)").bitcast(U32)
            nc.vector.tensor_copy(
                words.rearrange("p (s u) -> p u s", u=2)[:, u, :],
                x_pair[u][:].rearrange("p t e -> p (t e)").bitcast(U32).indirect(offsets[:, 8 * c : 8 * c + 8]),
            )

        def quant_x(c):
            nc.vector.quantize_mx(
                out=x_codes[:, c * C : (c + 1) * C].bitcast(FP8X4),
                scales=x_scales[:, c * C : (c + 1) * C],
                in_=x_slot[c][:].rearrange("p s d -> p (s d)"),
            )

        hidden, h_codes, h_scales, banks, results = {}, {}, {}, {}, {}

        def project(c, sub):
            e = (c, E)[sub]
            a = psum.tile([P, H], F32, name="a")
            b = psum.tile([P, H], F32, name="b")
            for bank, words, scales in ((a, w1w, w1s), (b, w3w, w3s)):
                nc.tensor.matmul_mx(
                    out=bank[:],
                    lhsT=x_codes[:, c * C : (c + 1) * C].bitcast(FP8X4),
                    lhsT_scale=x_scales[:, c * C : (c + 1) * C],
                    rhs=words[:, e, :].bitcast(FP4X4),
                    rhs_scale=scales[:, e * H : (e + 1) * H],
                    start=True,
                    stop=True,
                )
            banks[c, sub] = (a, b)

        def glu(c, sub):
            a, b = banks[c, sub]
            if sub == 0:
                hidden[c] = work.tile([P, 2, 2, P, 2], BF16, name="hidden", align_bytes=64)
            g = work.tile([P, 2, P, 2], F32, name="g")
            nc.scalar.activation(g[:], a[:].rearrange("s (q u e) -> s u q e", u=2, e=2), GELU)
            nc.vector.tensor_tensor(hidden[c][:, sub], g[:], b[:].rearrange("s (q u e) -> s u q e", u=2, e=2), MULT)

        def turn(c, lo, hi):
            m = hi - lo
            t = psum.tile([P, m, 2, C], F32, name="t")
            words = hidden[c][:].rearrange("s b u q e -> s (b u q e)").bitcast(F32)
            for sub in range(lo, hi):
                for u in range(2):
                    k = (2 * sub + u) * P
                    nc.tensor.transpose(t[:, sub - lo, u, :], words[:, k : k + P], ident[:])
            grouped = work.tile([P, m, C, 4], BF16, name="grouped%d" % m, align_bytes=64)
            nc.scalar.copy(
                grouped[:].rearrange("p b s d -> p (b s d)").bitcast(F32).rearrange("p (b s u) -> p b s u", b=m, u=2),
                t[:].rearrange("p b u s -> p b s u"),
            )
            h_codes[c, lo] = grouped

        def quant_h(c, lo, hi):
            m = hi - lo
            codes = work.tile([P, m * C], U32, name="h_code%d" % m, align_bytes=64)
            scales = work.tile([P, m * C], U8, name="h_scale%d" % m, align_bytes=64)
            nc.vector.quantize_mx(
                out=codes[:].bitcast(FP8X4),
                scales=scales[:],
                in_=h_codes[c, lo][:].rearrange("p b s d -> p (b s d)"),
            )
            for sub in range(lo, hi):
                k = (sub - lo) * C
                h_codes[c, sub] = (codes[:, k : k + C], scales[:, k : k + C])

        def last_layer(c, lo, hi):
            if lo == 0:
                results[c] = psum.tile([P, 2, 2, C], F32, name="y")
            y = results[c]
            for sub in range(lo, hi):
                e = (c, E)[sub]
                codes, scales = h_codes[c, sub]
                for u in range(2):
                    nc.tensor.matmul_mx(
                        out=y[:, sub, u, :],
                        lhsT=w2w[:, e, 2 * u * P : 2 * (u + 1) * P].bitcast(FP4X4),
                        lhsT_scale=w2s[:, e * N + u * P : e * N + (u + 1) * P],
                        rhs=codes.bitcast(FP8X4),
                        rhs_scale=scales,
                        start=True,
                        stop=True,
                    )

        def combine(c):
            y = results[c]
            gcol = gates[:, c * C : (c + 1) * C].unsqueeze(1).to_broadcast([P, 2, C])
            gated = work.tile([P, 2, C], F32, name="gated")
            total = keep.tile([P, 2, C], F32, name="total%d" % c)
            if c in GP:
                y_sb = work.tile([P, 2, 2, C], F32, name="y_sb")
                nc.scalar.copy(y_sb[:], y[:])
                nc.gpsimd.tensor_tensor(gated[:], y_sb[:, 0], gcol, MULT)
                nc.gpsimd.tensor_tensor(total[:], gated[:], y_sb[:, 1], ADD)
            else:
                nc.vector.tensor_tensor(gated[:], y[:, 0], gcol, MULT)
                nc.vector.tensor_tensor(total[:], gated[:], y[:, 1], ADD)
            results[c] = total

        def scatter(c):
            for u in range(2):
                nc.vector.tensor_copy(window[u][:].indirect(offsets[:, 8 * c : 8 * c + 8]), results[c][:, u, :])

        gather(0, 0)
        cast(0)
        gather(0, 1)
        cast(1)
        quant_x(0)
        gather(1, 0)
        gather(1, 1)
        quant_x(1)
        gather(2, 0)
        gather(2, 1)
        quant_x(2)
        gather(3, 0)
        gather(3, 1)
        quant_x(3)
        project(0, 0)
        project(0, 1)
        glu(0, 0)
        project(1, 0)
        glu(0, 1)
        for c in range(E):
            pieces = ((0, 2),) if c < E - 1 else ((0, 1), (1, 2))
            for lo, hi in pieces:
                turn(c, lo, hi)
            if c + 1 < E:
                project(c + 1, 1)
                glu(c + 1, 0)
            for lo, hi in pieces:
                quant_h(c, lo, hi)
            if c + 2 < E:
                project(c + 2, 0)
            if c + 1 < E:
                glu(c + 1, 1)
            for lo, hi in pieces:
                last_layer(c, lo, hi)
            if c > 0:
                scatter(c - 1)
            combine(c)
        scatter(E - 1)
        for u in range(2):
            nc.sync.dma_start(out[u * P : (u + 1) * P, :], window[u][:])
